import numpy as np
import ml_dtypes


def mxq(x, axis, fmt="e4m3"):
    dtype, down = {"e4m3": (ml_dtypes.float8_e4m3fn, 7), "e5m2": (ml_dtypes.float8_e5m2, 14)}[fmt]
    v = np.moveaxis(np.asarray(x, np.float32).astype(ml_dtypes.bfloat16).astype(np.float64), axis, -1)
    blocks = v.reshape(v.shape[:-1] + (-1, 32))
    amax = np.abs(blocks).max(-1, keepdims=True)
    byte = np.maximum(np.where(amax > 0, np.frexp(amax)[1] - 1 + 127, 0) - down, 1)
    scale = np.exp2(byte - 127.0)
    codes = (blocks / scale).astype(np.float32).astype(dtype).astype(np.float64)
    return np.moveaxis((codes * scale).reshape(v.shape), -1, axis)


WIDE = False


def mx_kscale(k):
    if not WIDE:
        return np.ones(k)
    levels = np.array([24, -24, 12, -12, 0])
    if k % 512:
        return np.exp2(np.random.permutation(np.resize(levels, k // 32))).repeat(32)
    a = np.empty((k // 512, 16))
    for p in range(k // 512):
        a[p, :8] = np.random.permutation(np.resize(levels, 8))
        for g in range(8):
            far = levels[np.abs(levels - a[p, g]) >= 10]
            a[p, g + 8] = far[np.random.randint(len(far))]
    return np.exp2(a.ravel()).repeat(32)


def f64(x):
    return np.asarray(x).astype(np.float64)


E2M1 = np.array([0.0, 0.5, 1.0, 1.5, 2.0, 3.0, 4.0, 6.0, -0.0, -0.5, -1.0, -1.5, -2.0, -3.0, -4.0, -6.0])


def pack_weight(w, fmt):
    k, n = w.shape
    w = f64(np.asarray(w, np.float32).astype(ml_dtypes.bfloat16)).reshape(k // 32, 32, n)
    amax = np.abs(w).max(1)
    if fmt == "e4m3":
        byte = np.frexp(amax)[1] - 1 + 127 - 7
    else:
        mant, ex = np.frexp(amax / 6.0)
        byte = np.where(mant > 0.5, ex, ex - 1) + 127
    byte = np.clip(np.where(amax > 0, byte, 1), 1, 254)
    scaled = (w * np.exp2(127.0 - byte)[:, None, :]).reshape(k, n).astype(np.float32)
    by_word = np.ascontiguousarray(scaled.reshape(k // 512, 128, 4, n).transpose(0, 1, 3, 2))
    if fmt == "e4m3":
        words = by_word.astype(ml_dtypes.float8_e4m3fn).view(np.uint8)
    else:
        c = by_word.astype(ml_dtypes.float4_e2m1fn).view(np.uint8) & 0xF
        words = (c[..., 0::2] | (c[..., 1::2] << 4)).reshape(k // 512, 128, 2 * n)
    return np.ascontiguousarray(words), np.ascontiguousarray(byte.astype(np.uint8).reshape(k // 512, 16, n))


def unpack_weight(words, scales, fmt):
    g, _, n = scales.shape
    words = np.ascontiguousarray(words).reshape(g, 128, n, -1)
    if fmt == "e4m3":
        vals = words.view(ml_dtypes.float8_e4m3fn).astype(np.float64)
    else:
        nib = np.empty((g, 128, n, 4), np.uint8)
        nib[..., 0::2] = words & 0xF
        nib[..., 1::2] = words >> 4
        vals = E2M1[nib]
    vals = vals * np.repeat(np.exp2(scales.astype(np.float64) - 127.0), 8, axis=1)[..., None]
    return vals.transpose(0, 1, 3, 2).reshape(g * 512, n)


def planes(y):
    n, m = y.shape
    v = y.astype(np.float32).astype(ml_dtypes.bfloat16).astype(np.float64).reshape(n // 32, 32, m)
    top = np.abs(v).max(1)
    byte = np.clip(np.where(top > 0, np.frexp(top)[1] - 1 + 127 - 7, 1), 1, 254)
    codes = (v * np.exp2(127.0 - byte)[:, None, :]).reshape(n, m).astype(np.float32).astype(ml_dtypes.float8_e4m3fn).view(np.uint8)
    words = codes.reshape(n // 512, 128, 4, m).transpose(0, 1, 3, 2)
    return np.ascontiguousarray(words), np.ascontiguousarray(byte.astype(np.uint8).reshape(n // 512, 16, m))


K, R, M, N, T = 1536, 512, 512, 1024, 1024


def setup_inputs():
    n = np.random.standard_normal
    u = mx_kscale(R)[:, None]
    s = mx_kscale(K)[:, None]
    p_wk = pack_weight(n((R, M)) / np.sqrt(R) / u, "e4m3")
    p_wv = pack_weight(n((R, N)) / np.sqrt(R) / u, "e4m3")
    return {
        "x": (n((K, T)) * s).astype(np.float32),
        "w": (n((K, R)) / np.sqrt(K) / s * u.T).astype(np.float32),
        "wk_words": p_wk[0],
        "wk_scales": p_wk[1],
        "wv_words": p_wv[0],
        "wv_scales": p_wv[1],
    }


def reference(x, w, wk_words, wk_scales, wv_words, wv_scales):
    x_ = mxq(f64(x), 0, "e4m3")
    w_ = mxq(f64(w), 0, "e4m3")
    c = w_.T @ x_
    c_ = mxq(c, 0, "e4m3")
    wk_ = unpack_weight(wk_words, wk_scales, "e4m3")
    wv_ = unpack_weight(wv_words, wv_scales, "e4m3")
    kk = wk_.T @ c_
    vv = wv_.T @ c_
    return (kk, vv, c) + planes(c)

@@ -1,0 +1,217 @@
+from contextlib import ExitStack
+
+import concourse.mybir as mybir
+
+K, R, M, N, T = 1536, 512, 512, 1024, 1024
+FLOPS = 2 * K * R * T + 2 * R * (M + N) * T
+
+F32 = mybir.dt.float32
+BF16 = mybir.dt.bfloat16
+I32 = mybir.dt.int32
+U32 = mybir.dt.uint32
+U8 = mybir.dt.uint8
+FP8X4 = mybir.dt.float8_e4m3fn_x4
+
+P = 128
+PACK = 4
+K_PASS = P * PACK
+PASSES = K // K_PASS
+HALF = 512
+GROUP = 4
+VECTOR_COLS = 320
+
+
+def tile_mix_mla_kernel(
+    tc, x, w, wk_words, wk_scales, wv_words, wv_scales, out_0, out_1, out_2, out_3, out_4
+):
+    nc = tc.nc
+    with ExitStack() as ctx:
+        sb = ctx.enter_context(tc.tile_pool(name="sb", bufs=1))
+        psum = ctx.enter_context(tc.psum_pool(name="psum", bufs=1))
+        ctx.enter_context(tc.manual_schedule())
+
+        def raw_tile(name):
+            return sb.tile([P, PACK, HALF], F32, name=name)
+
+        def load(rows, name):
+            raw = raw_tile(name)
+            nc.sync.dma_start(out=raw[:], in_=rows.rearrange("(p j) c -> p j c", j=PACK))
+            return raw
+
+        def k_rows(a):
+            return slice(a * K_PASS, (a + 1) * K_PASS)
+
+        def t_cols(h):
+            return slice(h * HALF, (h + 1) * HALF)
+
+        up_codes = sb.tile([P, M + N], U32, name="up_codes", align_bytes=64)
+        up_scales = sb.tile([P, M + N], U8, name="up_scales", align_bytes=64)
+        nc.gpsimd.memset(up_scales[:].bitcast(I32), 0)
+        for src, c0, c1 in ((wk_scales, 0, M), (wv_scales, M, M + N)):
+            for q in range(4):
+                nc.gpsimd.dma_start(
+                    out=up_scales[32 * q : 32 * q + 4, c0:c1].bitcast(I32),
+                    in_=src[0, 4 * q : 4 * q + 4, :].bitcast(I32),
+                )
+
+        w_raw, x_raw = {}, {}
+
+        def load_w(a):
+            w_raw[a] = load(w[k_rows(a), :], "w_raw%d" % a)
+
+        def load_x(h, a):
+            x_raw[h, a] = load(x[k_rows(a), t_cols(h)], "x_raw%d%d" % (h, a))
+
+        def load_words(src, c0, c1):
+            nc.sync.dma_start(
+                out=up_codes[:, c0:c1].bitcast(I32),
+                in_=src[0].rearrange("p n i -> p (n i)").bitcast(I32),
+            )
+
+        load_w(0)
+        load_x(0, 0)
+        load_w(1)
+        load_w(2)
+        load_x(0, 1)
+        load_x(0, 2)
+        load_x(1, 0)
+        load_x(1, 1)
+        load_words(wk_words, 0, M)
+        load_x(1, 2)
+        load_words(wv_words, M, M + N)
+
+        def copy(engine, out, in_):
+            if engine == "vector":
+                nc.vector.tensor_copy(out=out, in_=in_)
+            else:
+                nc.scalar.copy(out=out, in_=in_)
+
+        def shares(vector_cols):
+            both = (("vector", 0, vector_cols), ("scalar", vector_cols, HALF))
+            return [s for s in both if s[2] > s[1]]
+
+        def interleave(raw, name, vector_cols):
+            grouped = sb.tile([P, HALF * PACK], BF16, name=name, align_bytes=64)
+            for engine, c0, c1 in shares(vector_cols):
+                copy(
+                    engine,
+                    grouped[:, c0 * PACK : c1 * PACK].rearrange("p (c i j) -> p c j i", i=4, j=PACK),
+                    raw[:, :, c0:c1].rearrange("p j (c i) -> p c j i", i=4),
+                )
+            return grouped
+
+        def interleave_dealt(raw, name, vector_cols):
+            grouped = sb.tile([P, HALF * PACK], BF16, name=name, align_bytes=64)
+            for engine, c0, c1 in shares(vector_cols):
+                copy(
+                    engine,
+                    grouped[:].rearrange("p (s m j) -> p m s j", s=PACK, j=PACK)[:, c0 // PACK : c1 // PACK],
+                    raw[:, :, c0:c1].rearrange("p j (m s) -> p m s j", s=PACK),
+                )
+            return grouped
+
+        def quantize(grouped, codes, scales):
+            nc.vector.quantize_mx(out=codes.bitcast(FP8X4), scales=scales, in_=grouped[:])
+
+        def quantized(grouped, name):
+            codes = sb.tile([P, HALF], U32, name=name + "_codes", align_bytes=64)
+            scales = sb.tile([P, HALF], U8, name=name + "_scales", align_bytes=64)
+            quantize(grouped, codes[:], scales[:])
+            return codes, scales
+
+        def bank(b):
+            return psum.tile([P, HALF], F32, name="bank%d" % b)
+
+        def down_pass(banks, wq, xq, a):
+            for s in range(PACK):
+                cols = slice(s * P, (s + 1) * P)
+                nc.tensor.matmul_mx(
+                    out=banks[s][:],
+                    lhsT=wq[0][:, cols].bitcast(FP8X4),
+                    lhsT_scale=wq[1][:, cols],
+                    rhs=xq[0][:].bitcast(FP8X4),
+                    rhs_scale=xq[1][:],
+                    start=(a == 0),
+                    stop=(a == PASSES - 1),
+                )
+
+        c_codes = sb.tile([P, T], U32, name="c_codes", align_bytes=64)
+        c_scales = sb.tile([P, T], U8, name="c_scales", align_bytes=64)
+
+        def latent(banks, h, engines):
+            c_f32 = raw_tile("c_f32%d" % h)
+            for s in range(PACK):
+                copy(engines[s], c_f32[:, s, :], banks[s][:])
+            nc.sync.dma_start(out=out_2[:, t_cols(h)].rearrange("(p j) t -> p j t", j=PACK), in_=c_f32[:])
+            grouped = interleave(c_f32, "c_bf%d" % h, VECTOR_COLS)
+            quantize(grouped, c_codes[:, t_cols(h)], c_scales[:, t_cols(h)])
+            nc.sync.dma_start(
+                out=out_3[0].rearrange("p t i -> p (t i)").bitcast(I32)[:, t_cols(h)],
+                in_=c_codes[:, t_cols(h)].bitcast(I32),
+            )
+
+        staged = {}
+
+        def up_matmul(h, i, b):
+            acc = bank(b)
+            cols = slice(i * P, (i + 1) * P)
+            nc.tensor.matmul_mx(
+                out=acc[:],
+                lhsT=up_codes[:, cols].bitcast(FP8X4),
+                lhsT_scale=up_scales[:, cols],
+                rhs=c_codes[:, t_cols(h)].bitcast(FP8X4),
+                rhs_scale=c_scales[:, t_cols(h)],
+                start=True,
+                stop=True,
+            )
+            return acc
+
+        def up_drain(h, i, acc, engine):
+            g, u = divmod(i, GROUP)
+            if u == 0:
+                staged[h, g] = sb.tile([P, GROUP, HALF], F32, name="staged%d%d" % (h, g))
+            copy(engine, staged[h, g][:, u, :], acc[:])
+            if u == GROUP - 1:
+                rows = out_0 if g == 0 else out_1[(g - 1) * GROUP * P : g * GROUP * P, :]
+                nc.sync.dma_start(
+                    out=rows[:, t_cols(h)].rearrange("(u p) t -> p u t", p=P), in_=staged[h, g][:]
+                )
+
+        def up_tile(h, i, b, engine):
+            up_drain(h, i, up_matmul(h, i, b), engine)
+
+        wq = {}
+
+        def quantize_w(a):
+            wq[a] = quantized(interleave_dealt(w_raw[a], "w_bf%d" % a, VECTOR_COLS), "w%d" % a)
+
+        def quantized_x(h, a, vector_cols):
+            return quantized(interleave(x_raw[h, a], "x_bf%d%d" % (h, a), vector_cols), "x%d%d" % (h, a))
+
+        banks0 = [bank(s) for s in range(PACK)]
+        banks1 = [bank(PACK + s) for s in range(PACK)]
+        quantize_w(0)
+        down_pass(banks0, wq[0], quantized_x(0, 0, VECTOR_COLS), 0)
+        quantize_w(1)
+        quantize_w(2)
+        down_pass(banks0, wq[1], quantized_x(0, 1, VECTOR_COLS), 1)
+        down_pass(banks0, wq[2], quantized_x(0, 2, VECTOR_COLS), 2)
+        down_pass(banks1, wq[0], quantized_x(1, 0, HALF), 0)
+        latent(banks0, 0, ["scalar"] * PACK)
+        xq11 = quantized_x(1, 1, VECTOR_COLS)
+        xq12 = quantized_x(1, 2, HALF)
+        for i in range(2 * GROUP):
+            up_tile(0, i, i % PACK, "scalar")
+        down_pass(banks1, wq[1], xq11, 1)
+        down_pass(banks1, wq[2], xq12, 2)
+        held = [up_matmul(0, i, i % PACK) for i in range(2 * GROUP, 3 * GROUP)]
+        latent(banks1, 1, ["vector", "vector", "scalar", "scalar"])
+        for q in range(4):
+            nc.gpsimd.dma_start(
+                out=out_4[0, 4 * q : 4 * q + 4, :].bitcast(I32),
+                in_=c_scales[32 * q : 32 * q + 4, :].bitcast(I32),
+            )
+        for u, acc in enumerate(held):
+            up_drain(0, 2 * GROUP + u, acc, "scalar")
+        for i in range(3 * GROUP):
+            up_tile(1, i, (PACK + i) % (2 * PACK), "vector" if i < GROUP or i % 2 else "scalar")

@@ -17,8 +17,9 @@ PACK = 4
 K_PASS = P * PACK
 PASSES = K // K_PASS
 HALF = 512
-GROUP = 4
-VECTOR_COLS = 320
+LEAD = 2
+VECTOR_COLS = 288
+LATENT_VECTOR_COLS = 336
 
 
 def tile_mix_mla_kernel(
@@ -30,11 +31,8 @@ def tile_mix_mla_kernel(
         psum = ctx.enter_context(tc.psum_pool(name="psum", bufs=1))
         ctx.enter_context(tc.manual_schedule())
 
-        def raw_tile(name):
-            return sb.tile([P, PACK, HALF], F32, name=name)
-
         def load(rows, name):
-            raw = raw_tile(name)
+            raw = sb.tile([P, PACK, rows.shape[1]], F32, name=name)
             nc.sync.dma_start(out=raw[:], in_=rows.rearrange("(p j) c -> p j c", j=PACK))
             return raw
 
@@ -59,8 +57,12 @@ def tile_mix_mla_kernel(
         def load_w(a):
             w_raw[a] = load(w[k_rows(a), :], "w_raw%d" % a)
 
-        def load_x(h, a):
-            x_raw[h, a] = load(x[k_rows(a), t_cols(h)], "x_raw%d%d" % (h, a))
+        def load_x(a):
+            raw = load(x[k_rows(a), :], "x_raw%d" % a)
+            x_raw[a, 0], x_raw[a, 1] = (raw, 0), (raw, HALF)
+
+        def load_x_half(a, h):
+            x_raw[a, h] = (load(x[k_rows(a), t_cols(h)], "x_raw%d%d" % (a, h)), 0)
 
         def load_words(src, c0, c1):
             nc.sync.dma_start(
@@ -69,15 +71,15 @@ def tile_mix_mla_kernel(
             )
 
         load_w(0)
-        load_x(0, 0)
+        load_x_half(0, 0)
         load_w(1)
         load_w(2)
-        load_x(0, 1)
-        load_x(0, 2)
-        load_x(1, 0)
-        load_x(1, 1)
+        load_x_half(1, 0)
+        load_x_half(2, 0)
+        load_x_half(0, 1)
+        load_x_half(1, 1)
         load_words(wk_words, 0, M)
-        load_x(1, 2)
+        load_x_half(2, 1)
         load_words(wv_words, M, M + N)
 
         def copy(engine, out, in_):
@@ -90,13 +92,13 @@ def tile_mix_mla_kernel(
             both = (("vector", 0, vector_cols), ("scalar", vector_cols, HALF))
             return [s for s in both if s[2] > s[1]]
 
-        def interleave(raw, name, vector_cols):
+        def interleave(raw, t0, name, vector_cols):
             grouped = sb.tile([P, HALF * PACK], BF16, name=name, align_bytes=64)
             for engine, c0, c1 in shares(vector_cols):
                 copy(
                     engine,
-                    grouped[:, c0 * PACK : c1 * PACK].rearrange("p (c i j) -> p c j i", i=4, j=PACK),
-                    raw[:, :, c0:c1].rearrange("p j (c i) -> p c j i", i=4),
+                    grouped[:, c0 * PACK : c1 * PACK].rearrange("p (c i j) -> p c j i", i=2, j=PACK),
+                    raw[:, :, t0 + c0 : t0 + c1].rearrange("p j (c i) -> p c j i", i=2),
                 )
             return grouped
 
@@ -122,37 +124,81 @@ def tile_mix_mla_kernel(
         def bank(b):
             return psum.tile([P, HALF], F32, name="bank%d" % b)
 
-        def down_pass(banks, wq, xq, a):
+        xq, wq = {}, {}
+
+        def quantize_x(a, h, vector_cols=VECTOR_COLS):
+            name = "x%d%d" % (a, h)
+            xq[a, h] = quantized(interleave(*x_raw[a, h], name + "_bf", vector_cols), name)
+
+        def quantize_w(a):
+            grouped = interleave_dealt(w_raw[a], "w_bf%d" % a, VECTOR_COLS)
+            codes = sb.tile([P, R], U32, name="w%d_codes" % a, align_bytes=64)
+            scales = sb.tile([P, R], U8, name="w%d_scales" % a, align_bytes=64)
             for s in range(PACK):
                 cols = slice(s * P, (s + 1) * P)
-                nc.tensor.matmul_mx(
-                    out=banks[s][:],
-                    lhsT=wq[0][:, cols].bitcast(FP8X4),
-                    lhsT_scale=wq[1][:, cols],
-                    rhs=xq[0][:].bitcast(FP8X4),
-                    rhs_scale=xq[1][:],
-                    start=(a == 0),
-                    stop=(a == PASSES - 1),
+                nc.vector.quantize_mx(
+                    out=codes[:, cols].bitcast(FP8X4),
+                    scales=scales[:, cols],
+                    in_=grouped[:, s * K_PASS : (s + 1) * K_PASS],
                 )
+            wq[a] = (codes, scales)
 
+        c_banks = {(s, h): bank(h * PACK + s) for h in range(2) for s in range(PACK)}
+
+        def down(a, s, h):
+            cols = slice(s * P, (s + 1) * P)
+            nc.tensor.matmul_mx(
+                out=c_banks[s, h][:],
+                lhsT=wq[a][0][:, cols].bitcast(FP8X4),
+                lhsT_scale=wq[a][1][:, cols],
+                rhs=xq[a, h][0][:].bitcast(FP8X4),
+                rhs_scale=xq[a, h][1][:],
+                start=(a == 0),
+                stop=(a == PASSES - 1),
+            )
+
+        c_f32 = sb.tile([P, PACK, T], F32, name="c_f32")
         c_codes = sb.tile([P, T], U32, name="c_codes", align_bytes=64)
         c_scales = sb.tile([P, T], U8, name="c_scales", align_bytes=64)
 
-        def latent(banks, h, engines):
-            c_f32 = raw_tile("c_f32%d" % h)
-            for s in range(PACK):
-                copy(engines[s], c_f32[:, s, :], banks[s][:])
-            nc.sync.dma_start(out=out_2[:, t_cols(h)].rearrange("(p j) t -> p j t", j=PACK), in_=c_f32[:])
-            grouped = interleave(c_f32, "c_bf%d" % h, VECTOR_COLS)
-            quantize(grouped, c_codes[:, t_cols(h)], c_scales[:, t_cols(h)])
+        def drain_c(s, h, engine):
+            copy(engine, c_f32[:, s, t_cols(h)], c_banks[s, h][:])
+
+        def store_c(s0, s1, t0, t1):
             nc.sync.dma_start(
-                out=out_3[0].rearrange("p t i -> p (t i)").bitcast(I32)[:, t_cols(h)],
-                in_=c_codes[:, t_cols(h)].bitcast(I32),
+                out=out_2.rearrange("(p j) t -> p j t", j=PACK)[:, s0:s1, t0:t1], in_=c_f32[:, s0:s1, t0:t1]
             )
 
-        staged = {}
+        def store_codes(t0, t1):
+            nc.sync.dma_start(
+                out=out_3[0].rearrange("p t i -> p (t i)").bitcast(I32)[:, t0:t1],
+                in_=c_codes[:, t0:t1].bitcast(I32),
+            )
 
-        def up_matmul(h, i, b):
+        def store_scales():
+            for q in range(4):
+                nc.gpsimd.dma_start(
+                    out=out_4[0, 4 * q : 4 * q + 4, :].bitcast(I32),
+                    in_=c_scales[32 * q : 32 * q + 4, :].bitcast(I32),
+                )
+
+        def down_pass(a, h):
+            for s in range(PACK):
+                down(a, s, h)
+
+        def drain_latent(h, engines):
+            for s in range(PACK):
+                drain_c(s, h, engines[s])
+
+        def quantize_c(h, vector_cols):
+            grouped = interleave(c_f32, h * HALF, "c_bf%d" % h, vector_cols)
+            quantize(grouped, c_codes[:, t_cols(h)], c_scales[:, t_cols(h)])
+
+        up_tiles = (M + N) // P
+        staged = sb.tile([P, up_tiles, T], F32, name="staged")
+        pending = {}
+
+        def up_matmul(i, h, b):
             acc = bank(b)
             cols = slice(i * P, (i + 1) * P)
             nc.tensor.matmul_mx(
@@ -164,54 +210,57 @@ def tile_mix_mla_kernel(
                 start=True,
                 stop=True,
             )
-            return acc
+            pending[i, h] = acc
 
-        def up_drain(h, i, acc, engine):
-            g, u = divmod(i, GROUP)
-            if u == 0:
-                staged[h, g] = sb.tile([P, GROUP, HALF], F32, name="staged%d%d" % (h, g))
-            copy(engine, staged[h, g][:, u, :], acc[:])
-            if u == GROUP - 1:
-                rows = out_0 if g == 0 else out_1[(g - 1) * GROUP * P : g * GROUP * P, :]
-                nc.sync.dma_start(
-                    out=rows[:, t_cols(h)].rearrange("(u p) t -> p u t", p=P), in_=staged[h, g][:]
-                )
+        def up_drain(i, h, engine):
+            copy(engine, staged[:, i, t_cols(h)], pending[i, h][:])
 
-        def up_tile(h, i, b, engine):
-            up_drain(h, i, up_matmul(h, i, b), engine)
+        def up(i, h, b, engine):
+            up_matmul(i, h, b)
+            up_drain(i, h, engine)
 
-        wq = {}
+        def store_up(i0, i1, t0, t1):
+            out, first = (out_0, 0) if i0 < M // P else (out_1, M // P)
+            rows = out[(i0 - first) * P : (i1 - first) * P, t0:t1]
+            nc.sync.dma_start(out=rows.rearrange("(u p) t -> p u t", p=P), in_=staged[:, i0:i1, t0:t1])
 
-        def quantize_w(a):
-            wq[a] = quantized(interleave_dealt(w_raw[a], "w_bf%d" % a, VECTOR_COLS), "w%d" % a)
-
-        def quantized_x(h, a, vector_cols):
-            return quantized(interleave(x_raw[h, a], "x_bf%d%d" % (h, a), vector_cols), "x%d%d" % (h, a))
-
-        banks0 = [bank(s) for s in range(PACK)]
-        banks1 = [bank(PACK + s) for s in range(PACK)]
+        S, V = "scalar", "vector"
         quantize_w(0)
-        down_pass(banks0, wq[0], quantized_x(0, 0, VECTOR_COLS), 0)
+        quantize_x(0, 0, 320)
+        down_pass(0, 0)
         quantize_w(1)
         quantize_w(2)
-        down_pass(banks0, wq[1], quantized_x(0, 1, VECTOR_COLS), 1)
-        down_pass(banks0, wq[2], quantized_x(0, 2, VECTOR_COLS), 2)
-        down_pass(banks1, wq[0], quantized_x(1, 0, HALF), 0)
-        latent(banks0, 0, ["scalar"] * PACK)
-        xq11 = quantized_x(1, 1, VECTOR_COLS)
-        xq12 = quantized_x(1, 2, HALF)
-        for i in range(2 * GROUP):
-            up_tile(0, i, i % PACK, "scalar")
-        down_pass(banks1, wq[1], xq11, 1)
-        down_pass(banks1, wq[2], xq12, 2)
-        held = [up_matmul(0, i, i % PACK) for i in range(2 * GROUP, 3 * GROUP)]
-        latent(banks1, 1, ["vector", "vector", "scalar", "scalar"])
-        for q in range(4):
-            nc.gpsimd.dma_start(
-                out=out_4[0, 4 * q : 4 * q + 4, :].bitcast(I32),
-                in_=c_scales[32 * q : 32 * q + 4, :].bitcast(I32),
-            )
-        for u, acc in enumerate(held):
-            up_drain(0, 2 * GROUP + u, acc, "scalar")
-        for i in range(3 * GROUP):
-            up_tile(1, i, (PACK + i) % (2 * PACK), "vector" if i < GROUP or i % 2 else "scalar")
+        quantize_x(1, 0, 320)
+        down_pass(1, 0)
+        quantize_x(2, 0, 320)
+        down_pass(2, 0)
+        quantize_x(0, 1, HALF)
+        down_pass(0, 1)
+        drain_latent(0, [S, S, S, S])
+        store_c(0, 4, 0, HALF)
+        quantize_c(0, 320)
+        store_codes(0, HALF)
+        quantize_x(1, 1, 320)
+        quantize_x(2, 1, HALF)
+        for i in range(4):
+            up(i, 0, i, S)
+        store_up(0, 4, 0, HALF)
+        down_pass(1, 1)
+        for i in range(4, 8):
+            up(i, 0, i % 4, S)
+        store_up(4, 8, 0, HALF)
+        down_pass(2, 1)
+        for i in range(8, 12):
+            up_matmul(i, 0, i % 4)
+        drain_latent(1, [V, V, V, S])
+        store_c(0, 4, HALF, T)
+        quantize_c(1, 320)
+        store_codes(HALF, T)
+        store_scales()
+        for i in range(8, 12):
+            up_drain(i, 0, S)
+        ends = {3: (0, 4, HALF), 7: (4, 8, HALF), 11: (8, 12, 0)}
+        for i in range(12):
+            up(i, 1, (4 + i) % 8, V if i < 4 or i % 2 else S)
+            if i in ends:
+                store_up(*ends[i], T)

@@ -44,10 +44,11 @@ def tile_mix_mla_kernel(
 
         up_codes = sb.tile([P, M + N], U32, name="up_codes", align_bytes=64)
         up_scales = sb.tile([P, M + N], U8, name="up_scales", align_bytes=64)
-        nc.gpsimd.memset(up_scales[:].bitcast(I32), 0)
-        for src, c0, c1 in ((wk_scales, 0, M), (wv_scales, M, M + N)):
+        nc.vector.memset(up_scales[:].bitcast(I32), 0)
+
+        def load_scales(src, c0, c1):
             for q in range(4):
-                nc.gpsimd.dma_start(
+                nc.sync.dma_start(
                     out=up_scales[32 * q : 32 * q + 4, c0:c1].bitcast(I32),
                     in_=src[0, 4 * q : 4 * q + 4, :].bitcast(I32),
                 )
@@ -73,10 +74,12 @@ def tile_mix_mla_kernel(
         load_w(0)
         load_x_half(0, 0)
         load_w(1)
+        load_scales(wk_scales, 0, M)
         load_w(2)
         load_x_half(1, 0)
         load_x_half(2, 0)
         load_x_half(0, 1)
+        load_scales(wv_scales, M, M + N)
         load_x_half(1, 1)
         load_words(wk_words, 0, M)
         load_x_half(2, 1)
@@ -177,7 +180,7 @@ def tile_mix_mla_kernel(
 
         def store_scales():
             for q in range(4):
-                nc.gpsimd.dma_start(
+                nc.sync.dma_start(
                     out=out_4[0, 4 * q : 4 * q + 4, :].bitcast(I32),
                     in_=c_scales[32 * q : 32 * q + 4, :].bitcast(I32),
                 )
@@ -256,7 +259,6 @@ def tile_mix_mla_kernel(
         store_c(0, 4, HALF, T)
         quantize_c(1, 320)
         store_codes(HALF, T)
-        store_scales()
         for i in range(8, 12):
             up_drain(i, 0, S)
         ends = {3: (0, 4, HALF), 7: (4, 8, HALF), 11: (8, 12, 0)}
@@ -264,3 +266,5 @@ def tile_mix_mla_kernel(
             up(i, 1, (4 + i) % 8, V if i < 4 or i % 2 else S)
             if i in ends:
                 store_up(*ends[i], T)
+            if i == 3:
+                store_scales()

@@ -15,11 +15,13 @@ FP8X4 = mybir.dt.float8_e4m3fn_x4
 P = 128
 PACK = 4
 K_PASS = P * PACK
-PASSES = K // K_PASS
 HALF = 512
-LEAD = 2
-VECTOR_COLS = 288
-LATENT_VECTOR_COLS = 336
+QUADRANTS = 4
+GROUP = 4
+VECTOR_COLS = 320
+VECTOR_COLS_W = 288
+SCALAR, VECTOR = "scalar", "vector"
+ALTERNATE = (SCALAR, VECTOR, SCALAR, VECTOR)
 
 
 def tile_mix_mla_kernel(
@@ -30,11 +32,6 @@ def tile_mix_mla_kernel(
         sb = ctx.enter_context(tc.tile_pool(name="sb", bufs=1))
         psum = ctx.enter_context(tc.psum_pool(name="psum", bufs=1))
         ctx.enter_context(tc.manual_schedule())
-
-        def load(rows, name):
-            raw = sb.tile([P, PACK, rows.shape[1]], F32, name=name)
-            nc.sync.dma_start(out=raw[:], in_=rows.rearrange("(p j) c -> p j c", j=PACK))
-            return raw
 
         def k_rows(a):
             return slice(a * K_PASS, (a + 1) * K_PASS)
@@ -47,23 +44,11 @@ def tile_mix_mla_kernel(
         nc.vector.memset(up_scales[:].bitcast(I32), 0)
 
         def load_scales(src, c0, c1):
-            for q in range(4):
+            for q in range(QUADRANTS):
                 nc.sync.dma_start(
                     out=up_scales[32 * q : 32 * q + 4, c0:c1].bitcast(I32),
                     in_=src[0, 4 * q : 4 * q + 4, :].bitcast(I32),
                 )
-
-        w_raw, x_raw = {}, {}
-
-        def load_w(a):
-            w_raw[a] = load(w[k_rows(a), :], "w_raw%d" % a)
-
-        def load_x(a):
-            raw = load(x[k_rows(a), :], "x_raw%d" % a)
-            x_raw[a, 0], x_raw[a, 1] = (raw, 0), (raw, HALF)
-
-        def load_x_half(a, h):
-            x_raw[a, h] = (load(x[k_rows(a), t_cols(h)], "x_raw%d%d" % (a, h)), 0)
 
         def load_words(src, c0, c1):
             nc.sync.dma_start(
@@ -71,29 +56,42 @@ def tile_mix_mla_kernel(
                 in_=src[0].rearrange("p n i -> p (n i)").bitcast(I32),
             )
 
-        load_w(0)
-        load_x_half(0, 0)
-        load_w(1)
+        w_raw, x_raw = {}, {}
+
+        def load_rows(rows, name, queue):
+            raw = sb.tile([P, PACK, HALF], F32, name=name)
+            queue.dma_start(out=raw[:], in_=rows.rearrange("(p j) c -> p j c", j=PACK))
+            return raw
+
+        def load_w(a, queue):
+            w_raw[a] = load_rows(w[k_rows(a), :], "w_raw%d" % a, queue)
+
+        def load_x(a, h, queue):
+            x_raw[a, h] = load_rows(x[k_rows(a), t_cols(h)], "x_raw%d%d" % (a, h), queue)
+
+        load_w(0, nc.sync)
+        load_x(0, 0, nc.scalar)
+        load_w(1, nc.sync)
         load_scales(wk_scales, 0, M)
-        load_w(2)
-        load_x_half(1, 0)
-        load_x_half(2, 0)
-        load_x_half(0, 1)
+        load_w(2, nc.scalar)
+        load_x(1, 0, nc.sync)
+        load_x(2, 0, nc.sync)
+        load_x(0, 1, nc.sync)
         load_scales(wv_scales, M, M + N)
-        load_x_half(1, 1)
+        load_x(1, 1, nc.sync)
         load_words(wk_words, 0, M)
-        load_x_half(2, 1)
         load_words(wv_words, M, M + N)
+        load_x(2, 1, nc.sync)
 
         def copy(engine, out, in_):
-            if engine == "vector":
+            if engine == VECTOR:
                 nc.vector.tensor_copy(out=out, in_=in_)
             else:
                 nc.scalar.copy(out=out, in_=in_)
 
         def shares(vector_cols):
-            both = (("vector", 0, vector_cols), ("scalar", vector_cols, HALF))
-            return [s for s in both if s[2] > s[1]]
+            both = ((VECTOR, 0, vector_cols), (SCALAR, vector_cols, HALF))
+            return [share for share in both if share[2] > share[1]]
 
         def interleave(raw, t0, name, vector_cols):
             grouped = sb.tile([P, HALF * PACK], BF16, name=name, align_bytes=64)
@@ -105,107 +103,84 @@ def tile_mix_mla_kernel(
                 )
             return grouped
 
-        def interleave_dealt(raw, name, vector_cols):
-            grouped = sb.tile([P, HALF * PACK], BF16, name=name, align_bytes=64)
-            for engine, c0, c1 in shares(vector_cols):
-                copy(
-                    engine,
-                    grouped[:].rearrange("p (s m j) -> p m s j", s=PACK, j=PACK)[:, c0 // PACK : c1 // PACK],
-                    raw[:, :, c0:c1].rearrange("p j (m s) -> p m s j", s=PACK),
-                )
-            return grouped
-
         def quantize(grouped, codes, scales):
-            nc.vector.quantize_mx(out=codes.bitcast(FP8X4), scales=scales, in_=grouped[:])
-
-        def quantized(grouped, name):
-            codes = sb.tile([P, HALF], U32, name=name + "_codes", align_bytes=64)
-            scales = sb.tile([P, HALF], U8, name=name + "_scales", align_bytes=64)
-            quantize(grouped, codes[:], scales[:])
-            return codes, scales
-
-        def bank(b):
-            return psum.tile([P, HALF], F32, name="bank%d" % b)
+            nc.vector.quantize_mx(out=codes.bitcast(FP8X4), scales=scales, in_=grouped)
 
         xq, wq = {}, {}
 
-        def quantize_x(a, h, vector_cols=VECTOR_COLS):
+        def quantize_x(a, h, vector_cols):
             name = "x%d%d" % (a, h)
-            xq[a, h] = quantized(interleave(*x_raw[a, h], name + "_bf", vector_cols), name)
+            grouped = interleave(x_raw[a, h], 0, name + "_bf", vector_cols)
+            codes = sb.tile([P, HALF], U32, name=name + "_codes", align_bytes=64)
+            scales = sb.tile([P, HALF], U8, name=name + "_scales", align_bytes=64)
+            quantize(grouped[:], codes[:], scales[:])
+            xq[a, h] = (codes, scales)
 
         def quantize_w(a):
-            grouped = interleave_dealt(w_raw[a], "w_bf%d" % a, VECTOR_COLS)
+            grouped = sb.tile([P, R * PACK], BF16, name="w_bf%d" % a, align_bytes=64)
+            for engine, c0, c1 in shares(VECTOR_COLS_W):
+                copy(
+                    engine,
+                    grouped[:].rearrange("p (s m j) -> p m s j", s=PACK, j=PACK)[:, c0 // PACK : c1 // PACK],
+                    w_raw[a][:, :, c0:c1].rearrange("p j (m s) -> p m s j", s=PACK),
+                )
             codes = sb.tile([P, R], U32, name="w%d_codes" % a, align_bytes=64)
             scales = sb.tile([P, R], U8, name="w%d_scales" % a, align_bytes=64)
             for s in range(PACK):
                 cols = slice(s * P, (s + 1) * P)
-                nc.vector.quantize_mx(
-                    out=codes[:, cols].bitcast(FP8X4),
-                    scales=scales[:, cols],
-                    in_=grouped[:, s * K_PASS : (s + 1) * K_PASS],
-                )
+                quantize(grouped[:, s * K_PASS : (s + 1) * K_PASS], codes[:, cols], scales[:, cols])
             wq[a] = (codes, scales)
+
+        def bank(b):
+            return psum.tile([P, HALF], F32, name="bank%d" % b)
 
         c_banks = {(s, h): bank(h * PACK + s) for h in range(2) for s in range(PACK)}
 
-        def down(a, s, h):
-            cols = slice(s * P, (s + 1) * P)
-            nc.tensor.matmul_mx(
-                out=c_banks[s, h][:],
-                lhsT=wq[a][0][:, cols].bitcast(FP8X4),
-                lhsT_scale=wq[a][1][:, cols],
-                rhs=xq[a, h][0][:].bitcast(FP8X4),
-                rhs_scale=xq[a, h][1][:],
-                start=(a == 0),
-                stop=(a == PASSES - 1),
-            )
+        def down_pass(a, h):
+            for s in range(PACK):
+                cols = slice(s * P, (s + 1) * P)
+                nc.tensor.matmul_mx(
+                    out=c_banks[s, h][:],
+                    lhsT=wq[a][0][:, cols].bitcast(FP8X4),
+                    lhsT_scale=wq[a][1][:, cols],
+                    rhs=xq[a, h][0][:].bitcast(FP8X4),
+                    rhs_scale=xq[a, h][1][:],
+                    start=(a == 0),
+                    stop=(a == K // K_PASS - 1),
+                )
 
         c_f32 = sb.tile([P, PACK, T], F32, name="c_f32")
         c_codes = sb.tile([P, T], U32, name="c_codes", align_bytes=64)
         c_scales = sb.tile([P, T], U8, name="c_scales", align_bytes=64)
 
-        def drain_c(s, h, engine):
-            copy(engine, c_f32[:, s, t_cols(h)], c_banks[s, h][:])
-
-        def store_c(s0, s1, t0, t1):
+        def finish_latent(h, engines):
+            for s in range(PACK):
+                copy(engines[s], c_f32[:, s, t_cols(h)], c_banks[s, h][:])
             nc.sync.dma_start(
-                out=out_2.rearrange("(p j) t -> p j t", j=PACK)[:, s0:s1, t0:t1], in_=c_f32[:, s0:s1, t0:t1]
+                out=out_2.rearrange("(p j) t -> p j t", j=PACK)[:, :, t_cols(h)], in_=c_f32[:, :, t_cols(h)]
+            )
+            grouped = interleave(c_f32, h * HALF, "c_bf%d" % h, VECTOR_COLS)
+            quantize(grouped[:], c_codes[:, t_cols(h)], c_scales[:, t_cols(h)])
+            nc.sync.dma_start(
+                out=out_3[0].rearrange("p t i -> p (t i)").bitcast(I32)[:, t_cols(h)],
+                in_=c_codes[:, t_cols(h)].bitcast(I32),
             )
 
-        def store_codes(t0, t1):
-            nc.sync.dma_start(
-                out=out_3[0].rearrange("p t i -> p (t i)").bitcast(I32)[:, t0:t1],
-                in_=c_codes[:, t0:t1].bitcast(I32),
-            )
-
-        def store_scales():
-            for q in range(4):
+        def store_latent_scales():
+            for q in range(QUADRANTS):
                 nc.sync.dma_start(
                     out=out_4[0, 4 * q : 4 * q + 4, :].bitcast(I32),
                     in_=c_scales[32 * q : 32 * q + 4, :].bitcast(I32),
                 )
 
-        def down_pass(a, h):
-            for s in range(PACK):
-                down(a, s, h)
-
-        def drain_latent(h, engines):
-            for s in range(PACK):
-                drain_c(s, h, engines[s])
-
-        def quantize_c(h, vector_cols):
-            grouped = interleave(c_f32, h * HALF, "c_bf%d" % h, vector_cols)
-            quantize(grouped, c_codes[:, t_cols(h)], c_scales[:, t_cols(h)])
-
-        up_tiles = (M + N) // P
-        staged = sb.tile([P, up_tiles, T], F32, name="staged")
-        pending = {}
+        staged = sb.tile([P, (M + N) // P, T], F32, name="staged")
+        sums = {}
 
         def up_matmul(i, h, b):
-            acc = bank(b)
+            sums[i, h] = bank(b)
             cols = slice(i * P, (i + 1) * P)
             nc.tensor.matmul_mx(
-                out=acc[:],
+                out=sums[i, h][:],
                 lhsT=up_codes[:, cols].bitcast(FP8X4),
                 lhsT_scale=up_scales[:, cols],
                 rhs=c_codes[:, t_cols(h)].bitcast(FP8X4),
@@ -213,58 +188,62 @@ def tile_mix_mla_kernel(
                 start=True,
                 stop=True,
             )
-            pending[i, h] = acc
 
         def up_drain(i, h, engine):
-            copy(engine, staged[:, i, t_cols(h)], pending[i, h][:])
+            copy(engine, staged[:, i, t_cols(h)], sums[i, h][:])
 
         def up(i, h, b, engine):
             up_matmul(i, h, b)
             up_drain(i, h, engine)
 
-        def store_up(i0, i1, t0, t1):
-            out, first = (out_0, 0) if i0 < M // P else (out_1, M // P)
-            rows = out[(i0 - first) * P : (i1 - first) * P, t0:t1]
-            nc.sync.dma_start(out=rows.rearrange("(u p) t -> p u t", p=P), in_=staged[:, i0:i1, t0:t1])
+        def tiles(group):
+            return range(group * GROUP, (group + 1) * GROUP)
 
-        S, V = "scalar", "vector"
+        def store_group(group, cols, queue):
+            rows = out_0 if group == 0 else out_1[(group - 1) * GROUP * P : group * GROUP * P, :]
+            queue.dma_start(
+                out=rows[:, cols].rearrange("(u p) t -> p u t", p=P),
+                in_=staged[:, group * GROUP : (group + 1) * GROUP, cols],
+            )
+
         quantize_w(0)
-        quantize_x(0, 0, 320)
+        quantize_x(0, 0, VECTOR_COLS)
         down_pass(0, 0)
         quantize_w(1)
         quantize_w(2)
-        quantize_x(1, 0, 320)
-        down_pass(1, 0)
-        quantize_x(2, 0, 320)
-        down_pass(2, 0)
+        for a in (1, 2):
+            quantize_x(a, 0, VECTOR_COLS)
+            down_pass(a, 0)
+
         quantize_x(0, 1, HALF)
         down_pass(0, 1)
-        drain_latent(0, [S, S, S, S])
-        store_c(0, 4, 0, HALF)
-        quantize_c(0, 320)
-        store_codes(0, HALF)
-        quantize_x(1, 1, 320)
+        finish_latent(0, (SCALAR,) * PACK)
+
+        quantize_x(1, 1, VECTOR_COLS)
+        for i in tiles(0):
+            up(i, 0, i % PACK, VECTOR if i == GROUP - 1 else SCALAR)
+        store_group(0, t_cols(0), nc.sync)
         quantize_x(2, 1, HALF)
-        for i in range(4):
-            up(i, 0, i, S)
-        store_up(0, 4, 0, HALF)
+        for i in tiles(1):
+            up(i, 0, i % PACK, SCALAR)
+        store_group(1, t_cols(0), nc.sync)
         down_pass(1, 1)
-        for i in range(4, 8):
-            up(i, 0, i % 4, S)
-        store_up(4, 8, 0, HALF)
         down_pass(2, 1)
-        for i in range(8, 12):
-            up_matmul(i, 0, i % 4)
-        drain_latent(1, [V, V, V, S])
-        store_c(0, 4, HALF, T)
-        quantize_c(1, 320)
-        store_codes(HALF, T)
-        for i in range(8, 12):
-            up_drain(i, 0, S)
-        ends = {3: (0, 4, HALF), 7: (4, 8, HALF), 11: (8, 12, 0)}
-        for i in range(12):
-            up(i, 1, (4 + i) % 8, V if i < 4 or i % 2 else S)
-            if i in ends:
-                store_up(*ends[i], T)
-            if i == 3:
-                store_scales()
+
+        for i in tiles(2):
+            up_matmul(i, 0, i % PACK)
+        finish_latent(1, ALTERNATE[::-1])
+        for i in tiles(2)[:2]:
+            up_drain(i, 0, SCALAR)
+        for i in tiles(0):
+            up(i, 1, PACK + i % PACK, ALTERNATE[i % PACK])
+        store_group(0, t_cols(1), nc.sync)
+        store_latent_scales()
+        for i in tiles(2)[2:]:
+            up_drain(i, 0, SCALAR)
+        for i in tiles(1):
+            up(i, 1, PACK + i % PACK, VECTOR)
+        store_group(1, t_cols(1), nc.sync)
+        for i in tiles(2):
+            up(i, 1, i % PACK, ALTERNATE[i % PACK])
+        store_group(2, slice(0, T), nc.scalar)

from contextlib import ExitStack

import concourse.mybir as mybir

K, R, M, N, T = 1536, 512, 512, 1024, 1024
FLOPS = 2 * K * R * T + 2 * R * (M + N) * T

F32 = mybir.dt.float32
BF16 = mybir.dt.bfloat16
I32 = mybir.dt.int32
U32 = mybir.dt.uint32
U8 = mybir.dt.uint8
FP8X4 = mybir.dt.float8_e4m3fn_x4

P = 128
PACK = 4
K_PASS = P * PACK
HALF = 512
QUADRANTS = 4
GROUP = 4
VECTOR_COLS = 320
VECTOR_COLS_W = 288
SCALAR, VECTOR = "scalar", "vector"
ALTERNATE = (SCALAR, VECTOR, SCALAR, VECTOR)


def tile_mix_mla_kernel(
    tc, x, w, wk_words, wk_scales, wv_words, wv_scales, out_0, out_1, out_2, out_3, out_4
):
    nc = tc.nc
    with ExitStack() as ctx:
        sb = ctx.enter_context(tc.tile_pool(name="sb", bufs=1))
        psum = ctx.enter_context(tc.psum_pool(name="psum", bufs=1))
        ctx.enter_context(tc.manual_schedule())

        def k_rows(a):
            return slice(a * K_PASS, (a + 1) * K_PASS)

        def t_cols(h):
            return slice(h * HALF, (h + 1) * HALF)

        up_codes = sb.tile([P, M + N], U32, name="up_codes", align_bytes=64)
        up_scales = sb.tile([P, M + N], U8, name="up_scales", align_bytes=64)
        nc.vector.memset(up_scales[:].bitcast(I32), 0)

        def load_scales(src, c0, c1):
            for q in range(QUADRANTS):
                nc.sync.dma_start(
                    out=up_scales[32 * q : 32 * q + 4, c0:c1].bitcast(I32),
                    in_=src[0, 4 * q : 4 * q + 4, :].bitcast(I32),
                )

        def load_words(src, c0, c1):
            nc.sync.dma_start(
                out=up_codes[:, c0:c1].bitcast(I32),
                in_=src[0].rearrange("p n i -> p (n i)").bitcast(I32),
            )

        w_raw, x_raw = {}, {}

        def load_rows(rows, name, queue):
            raw = sb.tile([P, PACK, HALF], F32, name=name)
            queue.dma_start(out=raw[:], in_=rows.rearrange("(p j) c -> p j c", j=PACK))
            return raw

        def load_w(a, queue):
            w_raw[a] = load_rows(w[k_rows(a), :], "w_raw%d" % a, queue)

        def load_x(a, h, queue):
            x_raw[a, h] = load_rows(x[k_rows(a), t_cols(h)], "x_raw%d%d" % (a, h), queue)

        load_w(0, nc.sync)
        load_x(0, 0, nc.scalar)
        load_w(1, nc.sync)
        load_scales(wk_scales, 0, M)
        load_w(2, nc.scalar)
        load_x(1, 0, nc.sync)
        load_x(2, 0, nc.sync)
        load_x(0, 1, nc.sync)
        load_scales(wv_scales, M, M + N)
        load_x(1, 1, nc.sync)
        load_words(wk_words, 0, M)
        load_words(wv_words, M, M + N)
        load_x(2, 1, nc.sync)

        def copy(engine, out, in_):
            if engine == VECTOR:
                nc.vector.tensor_copy(out=out, in_=in_)
            else:
                nc.scalar.copy(out=out, in_=in_)

        def shares(vector_cols):
            both = ((VECTOR, 0, vector_cols), (SCALAR, vector_cols, HALF))
            return [share for share in both if share[2] > share[1]]

        def interleave(raw, t0, name, vector_cols):
            grouped = sb.tile([P, HALF * PACK], BF16, name=name, align_bytes=64)
            for engine, c0, c1 in shares(vector_cols):
                copy(
                    engine,
                    grouped[:, c0 * PACK : c1 * PACK].rearrange("p (c i j) -> p c j i", i=2, j=PACK),
                    raw[:, :, t0 + c0 : t0 + c1].rearrange("p j (c i) -> p c j i", i=2),
                )
            return grouped

        def quantize(grouped, codes, scales):
            nc.vector.quantize_mx(out=codes.bitcast(FP8X4), scales=scales, in_=grouped)

        xq, wq = {}, {}

        def quantize_x(a, h, vector_cols):
            name = "x%d%d" % (a, h)
            grouped = interleave(x_raw[a, h], 0, name + "_bf", vector_cols)
            codes = sb.tile([P, HALF], U32, name=name + "_codes", align_bytes=64)
            scales = sb.tile([P, HALF], U8, name=name + "_scales", align_bytes=64)
            quantize(grouped[:], codes[:], scales[:])
            xq[a, h] = (codes, scales)

        def quantize_w(a):
            grouped = sb.tile([P, R * PACK], BF16, name="w_bf%d" % a, align_bytes=64)
            for engine, c0, c1 in shares(VECTOR_COLS_W):
                copy(
                    engine,
                    grouped[:].rearrange("p (s m j) -> p m s j", s=PACK, j=PACK)[:, c0 // PACK : c1 // PACK],
                    w_raw[a][:, :, c0:c1].rearrange("p j (m s) -> p m s j", s=PACK),
                )
            codes = sb.tile([P, R], U32, name="w%d_codes" % a, align_bytes=64)
            scales = sb.tile([P, R], U8, name="w%d_scales" % a, align_bytes=64)
            for s in range(PACK):
                cols = slice(s * P, (s + 1) * P)
                quantize(grouped[:, s * K_PASS : (s + 1) * K_PASS], codes[:, cols], scales[:, cols])
            wq[a] = (codes, scales)

        def bank(b):
            return psum.tile([P, HALF], F32, name="bank%d" % b)

        c_banks = {(s, h): bank(h * PACK + s) for h in range(2) for s in range(PACK)}

        def down_pass(a, h):
            for s in range(PACK):
                cols = slice(s * P, (s + 1) * P)
                nc.tensor.matmul_mx(
                    out=c_banks[s, h][:],
                    lhsT=wq[a][0][:, cols].bitcast(FP8X4),
                    lhsT_scale=wq[a][1][:, cols],
                    rhs=xq[a, h][0][:].bitcast(FP8X4),
                    rhs_scale=xq[a, h][1][:],
                    start=(a == 0),
                    stop=(a == K // K_PASS - 1),
                )

        c_f32 = sb.tile([P, PACK, T], F32, name="c_f32")
        c_codes = sb.tile([P, T], U32, name="c_codes", align_bytes=64)
        c_scales = sb.tile([P, T], U8, name="c_scales", align_bytes=64)

        def finish_latent(h, engines):
            for s in range(PACK):
                copy(engines[s], c_f32[:, s, t_cols(h)], c_banks[s, h][:])
            nc.sync.dma_start(
                out=out_2.rearrange("(p j) t -> p j t", j=PACK)[:, :, t_cols(h)], in_=c_f32[:, :, t_cols(h)]
            )
            grouped = interleave(c_f32, h * HALF, "c_bf%d" % h, VECTOR_COLS)
            quantize(grouped[:], c_codes[:, t_cols(h)], c_scales[:, t_cols(h)])
            nc.sync.dma_start(
                out=out_3[0].rearrange("p t i -> p (t i)").bitcast(I32)[:, t_cols(h)],
                in_=c_codes[:, t_cols(h)].bitcast(I32),
            )

        def store_latent_scales():
            for q in range(QUADRANTS):
                nc.sync.dma_start(
                    out=out_4[0, 4 * q : 4 * q + 4, :].bitcast(I32),
                    in_=c_scales[32 * q : 32 * q + 4, :].bitcast(I32),
                )

        staged = sb.tile([P, (M + N) // P, T], F32, name="staged")
        sums = {}

        def up_matmul(i, h, b):
            sums[i, h] = bank(b)
            cols = slice(i * P, (i + 1) * P)
            nc.tensor.matmul_mx(
                out=sums[i, h][:],
                lhsT=up_codes[:, cols].bitcast(FP8X4),
                lhsT_scale=up_scales[:, cols],
                rhs=c_codes[:, t_cols(h)].bitcast(FP8X4),
                rhs_scale=c_scales[:, t_cols(h)],
                start=True,
                stop=True,
            )

        def up_drain(i, h, engine):
            copy(engine, staged[:, i, t_cols(h)], sums[i, h][:])

        def up(i, h, b, engine):
            up_matmul(i, h, b)
            up_drain(i, h, engine)

        def tiles(group):
            return range(group * GROUP, (group + 1) * GROUP)

        def store_group(group, cols, queue):
            rows = out_0 if group == 0 else out_1[(group - 1) * GROUP * P : group * GROUP * P, :]
            queue.dma_start(
                out=rows[:, cols].rearrange("(u p) t -> p u t", p=P),
                in_=staged[:, group * GROUP : (group + 1) * GROUP, cols],
            )

        quantize_w(0)
        quantize_x(0, 0, VECTOR_COLS)
        down_pass(0, 0)
        quantize_w(1)
        quantize_w(2)
        for a in (1, 2):
            quantize_x(a, 0, VECTOR_COLS)
            down_pass(a, 0)

        quantize_x(0, 1, HALF)
        down_pass(0, 1)
        finish_latent(0, (SCALAR,) * PACK)

        quantize_x(1, 1, VECTOR_COLS)
        for i in tiles(0):
            up(i, 0, i % PACK, VECTOR if i == GROUP - 1 else SCALAR)
        store_group(0, t_cols(0), nc.sync)
        quantize_x(2, 1, HALF)
        for i in tiles(1):
            up(i, 0, i % PACK, SCALAR)
        store_group(1, t_cols(0), nc.sync)
        down_pass(1, 1)
        down_pass(2, 1)

        for i in tiles(2):
            up_matmul(i, 0, i % PACK)
        finish_latent(1, ALTERNATE[::-1])
        for i in tiles(2)[:2]:
            up_drain(i, 0, SCALAR)
        for i in tiles(0):
            up(i, 1, PACK + i % PACK, ALTERNATE[i % PACK])
        store_group(0, t_cols(1), nc.sync)
        store_latent_scales()
        for i in tiles(2)[2:]:
            up_drain(i, 0, SCALAR)
        for i in tiles(1):
            up(i, 1, PACK + i % PACK, VECTOR)
        store_group(1, t_cols(1), nc.sync)
        for i in tiles(2):
            up(i, 1, i % PACK, ALTERNATE[i % PACK])
        store_group(2, slice(0, T), nc.scalar)
